import numpy as np
import ml_dtypes


def mxq(x, axis, fmt="e4m3"):
    dtype, down = {"e4m3": (ml_dtypes.float8_e4m3fn, 7), "e5m2": (ml_dtypes.float8_e5m2, 14)}[fmt]
    v = np.moveaxis(np.asarray(x, np.float32).astype(ml_dtypes.bfloat16).astype(np.float64), axis, -1)
    blocks = v.reshape(v.shape[:-1] + (-1, 32))
    amax = np.abs(blocks).max(-1, keepdims=True)
    byte = np.maximum(np.where(amax > 0, np.frexp(amax)[1] - 1 + 127, 0) - down, 1)
    scale = np.exp2(byte - 127.0)
    codes = (blocks / scale).astype(np.float32).astype(dtype).astype(np.float64)
    return np.moveaxis((codes * scale).reshape(v.shape), -1, axis)


WIDE = False


def mx_kscale(k):
    if not WIDE:
        return np.ones(k)
    levels = np.array([10, -10, 5, -5, 0])
    if k % 512:
        return np.exp2(np.random.permutation(np.resize(levels, k // 32))).repeat(32)
    a = np.empty((k // 512, 16))
    for p in range(k // 512):
        a[p, :8] = np.random.permutation(np.resize(levels, 8))
        for g in range(8):
            far = levels[np.abs(levels - a[p, g]) >= 10]
            a[p, g + 8] = far[np.random.randint(len(far))]
    return np.exp2(a.ravel()).repeat(32)


def f64(x):
    return np.asarray(x).astype(np.float64)


def striped(idx):
    return np.tile(idx.reshape(-1, 16).T, (8, 1)).astype(np.uint16)


def unstriped(offs):
    return offs[:16].T.reshape(-1).astype(np.int64)


def striped8(idx):
    return np.concatenate([x.reshape(-1, 16).T for x in idx]).astype(np.uint16)


def runs(offs, k):
    lists = np.stack([offs[16 * r : 16 * r + 16].T.reshape(-1) for r in range(8)]).astype(np.int64)
    return lists[np.arange(k) % 512 // 64]


def pack_weight(w):
    k, n = w.shape
    w = f64(np.asarray(w, np.float32).astype(ml_dtypes.bfloat16)).reshape(k // 32, 32, n)
    amax = np.abs(w).max(1)
    byte = np.clip(np.where(amax > 0, np.frexp(amax)[1] - 1 + 127 - 7, 1), 1, 254)
    scaled = (w * np.exp2(127.0 - byte)[:, None, :]).reshape(k, n).astype(np.float32)
    words = np.ascontiguousarray(scaled.reshape(k // 512, 128, 4, n).transpose(0, 1, 3, 2)).astype(ml_dtypes.float8_e4m3fn).view(np.uint8)
    return words, np.ascontiguousarray(byte.astype(np.uint8).reshape(k // 512, 16, n))


def unpack_weight(words, scales):
    g, p, n, _ = words.shape
    vals = np.ascontiguousarray(words).view(ml_dtypes.float8_e4m3fn).astype(np.float64) * np.repeat(np.exp2(scales.astype(np.float64) - 127.0), 8, axis=1)[..., None]
    return vals.transpose(0, 1, 3, 2).reshape(g * 512, n)


def sigmoid(v):
    return 1.0 / (1.0 + np.exp(-np.maximum(v, -700.0)))


K, T, S, H = 512, 2048, 512, 512


def setup_inputs():
    n = np.random.standard_normal
    s = mx_kscale(K)[:, None]
    u = mx_kscale(H)
    packed_xT = pack_weight(n((K, T)) * s)
    return {
        "x_words": packed_xT[0],
        "x_scales": packed_xT[1],
        "w1": (n((K, H)) / np.sqrt(K) / s).astype(np.float32),
        "gn": (np.random.uniform(0.5, 1.5, (H, 1)) * u[:, None]).astype(np.float32),
        "w2": (n((H, H)) / np.sqrt(H) / u[:, None]).astype(np.float32),
        "offs": striped(np.random.permutation(T)[:S]),
        "n1": striped8(np.stack([np.random.permutation(S) for _ in range(8)])),
        "n2": striped8(np.stack([np.random.permutation(S) for _ in range(8)])),
        "n3": striped8(np.stack([np.random.permutation(S) for _ in range(8)])),
        "n4": striped8(np.stack([np.random.permutation(S) for _ in range(8)])),
        "n5": striped8(np.stack([np.random.permutation(S) for _ in range(8)])),
        "n6": striped8(np.stack([np.random.permutation(S) for _ in range(8)])),
        "n7": striped8(np.stack([np.random.permutation(S) for _ in range(8)])),
    }


def reference(x_words, x_scales, w1, gn, w2, offs, n1, n2, n3, n4, n5, n6, n7):
    xq = unpack_weight(x_words, x_scales)[:, unstriped(offs)]
    y = mxq(f64(w1), 0, "e4m3").T @ xq
    pa = y[np.arange(H)[:, None], runs(n1, H)]
    pb = y[np.arange(H)[:, None], runs(n2, H)]
    z = f64(gn) * (np.maximum(np.minimum(y, pa), np.minimum(np.maximum(y, pa), pb)))
    w2q = mxq(f64(w2), 0, "e4m3")
    a = w2q.T @ mxq(z, 0, "e4m3")
    pa2 = y[np.arange(H)[:, None], runs(n3, H)]
    z2 = f64(gn) * (pa2 + (sigmoid(y[np.arange(H)[:, None], runs(n4, H)])) * (y[np.arange(H)[:, None], runs(n5, H)] - pa2))
    b = w2q.T @ mxq(z2, 0, "e4m3")
    return a + (sigmoid(b[np.arange(H)[:, None], runs(n7, H)] - b)) * (a[np.arange(H)[:, None], runs(n6, H)] - a)

@@ -1,0 +1,297 @@
+from contextlib import ExitStack
+
+import concourse.mybir as mybir
+from concourse.masks import make_identity
+
+F32 = mybir.dt.float32
+BF16 = mybir.dt.bfloat16
+I32 = mybir.dt.int32
+U32 = mybir.dt.uint32
+U16 = mybir.dt.uint16
+U8 = mybir.dt.uint8
+FP8X4 = mybir.dt.float8_e4m3fn_x4
+ALU = mybir.AluOpType
+ACT = mybir.ActivationFunctionType
+
+P = 128
+PACK = 4
+T = 2048
+S = 512
+H = 512
+HALF = S // 2
+FLOPS = 3 * 2 * 512 * 512 * 512
+
+
+def cols(h):
+    return slice(h * HALF, (h + 1) * HALF)
+
+
+def entries(lst, h):
+    return lst[:, h * (HALF // 16) : (h + 1) * (HALF // 16)]
+
+
+def tile_picked_tiepullbmedlerp_none_p_kernel(
+    tc, x_words, x_scales, w1, gn, w2, offs, n1, n2, n3, n4, n5, n6, n7, out
+):
+    nc = tc.nc
+    with ExitStack() as ctx:
+        lists = ctx.enter_context(tc.tile_pool(name="lists", bufs=1))
+        keep = ctx.enter_context(tc.tile_pool(name="keep", bufs=1))
+        psum = ctx.enter_context(tc.psum_pool(name="psum", bufs=1))
+
+        def bank(i):
+            return psum.tile([P, S], F32, name="bank%d" % i)
+
+        def load_list(name, src):
+            tile = lists.tile([P, S // 16], U16, name=name)
+            nc.sync.dma_start(tile[:], src)
+            return tile
+
+        def f32_tiles(name, width):
+            return [keep.tile([P, width], F32, name="%s%d" % (name, t), align_bytes=64) for t in range(PACK)]
+
+        warm = keep.tile([P, 1], F32, name="warm")
+        warm2 = keep.tile([P, 1], F32, name="warm2")
+        nc.vector.memset(warm[:], 0.0)
+        nc.scalar.activation(warm2[:], warm[:], ACT.Sigmoid)
+
+        xs = keep.tile([P, T], U8, name="xs", align_bytes=64)
+        nc.vector.memset(xs[:].bitcast(I32), 0)
+        w1_raw = keep.tile([P, PACK, H], F32, name="w1_raw")
+        nc.sync.dma_start(w1_raw[:], w1.rearrange("(p j) c -> p j c", j=PACK))
+        for q in range(4):
+            nc.scalar.dma_start(xs[32 * q : 32 * q + 4, :].bitcast(I32), x_scales[0, 4 * q : 4 * q + 4, :].bitcast(I32))
+        l_offs = load_list("l_offs", offs)
+        xw = keep.tile([P, T], U32, name="xw", align_bytes=64)
+        nc.sync.dma_start(xw[:].bitcast(I32), x_words[0].rearrange("p n t -> p (n t)").bitcast(I32))
+        gain = keep.tile([P, PACK], F32, name="gain")
+        nc.sync.dma_start(gain[:], gn.rearrange("(p t) o -> p (t o)", t=PACK))
+        l1 = load_list("l1", n1)
+        l2 = load_list("l2", n2)
+        w2_raw = keep.tile([P, PACK, H], F32, name="w2_raw")
+        nc.sync.dma_start(w2_raw[:], w2.rearrange("(p j) c -> p j c", j=PACK))
+        l4 = load_list("l4", n4)
+        l3 = load_list("l3", n3)
+        l5 = load_list("l5", n5)
+        l6 = load_list("l6", n6)
+        l7 = load_list("l7", n7)
+
+        ident = keep.tile([P, P], F32, name="ident")
+        make_identity(nc, ident[:])
+
+        def dealt(name, raw, copy):
+            grouped = keep.tile([P, PACK * H], BF16, name=name, align_bytes=64)
+            copy(
+                grouped[:].rearrange("p (t m j) -> p m j t", t=PACK, j=PACK),
+                raw[:].rearrange("p j (m t) -> p m j t", t=PACK),
+            )
+            return grouped
+
+        def quantize(name, grouped, width):
+            codes = keep.tile([P, width], U32, name=name + "_c", align_bytes=64)
+            scales = keep.tile([P, width], U8, name=name + "_s", align_bytes=64)
+            nc.vector.quantize_mx(out=codes[:].bitcast(FP8X4), scales=scales[:], in_=grouped)
+            return codes, scales
+
+        def product(dst, w, t, codes, scales):
+            m = slice(t * P, (t + 1) * P)
+            nc.tensor.matmul_mx(
+                out=dst, lhsT=w[0][:, m].bitcast(FP8X4), lhsT_scale=w[1][:, m],
+                rhs=codes.bitcast(FP8X4), rhs_scale=scales, start=True, stop=True,
+            )
+
+        w1q = quantize("w1q", dealt("w1g", w1_raw, nc.vector.tensor_copy)[:], H)
+        xs_g = keep.tile([P, S], U8, name="xs_g", align_bytes=64)
+        nc.vector.tensor_copy(xs_g[:], xs[:].indirect(l_offs[:]))
+
+        ybank = [bank(i) for i in range(4)]
+        for h in range(2):
+            xw_g = keep.tile([P, HALF], U32, name="xw_g%d" % h, align_bytes=64)
+            nc.vector.tensor_copy(xw_g[:], xw[:].indirect(entries(l_offs, h)))
+            for t in range(PACK):
+                product(ybank[2 * h + t // 2][:, cols(t % 2)], w1q, t, xw_g[:], xs_g[:, cols(h)])
+
+        yg = f32_tiles("yg", S)
+        yg2 = f32_tiles("ygc", S)
+        y = f32_tiles("y", S)
+
+        def y_psum(t, h):
+            return ybank[2 * h + t // 2][:, cols(t % 2)]
+
+        def scaled(dst, t, h):
+            nc.scalar.activation(dst[t][:, cols(h)], y_psum(t, h), ACT.Copy, scale=gain[:, t : t + 1])
+
+        scaled(yg, 0, 0)
+        scaled(yg2, 0, 0)
+        scaled(yg, 0, 1)
+        scaled(yg2, 0, 1)
+        for h in range(2):
+            scaled(yg, 1, h)
+        for h in range(2):
+            scaled(yg2, 1, h)
+        for t in (2, 3):
+            for h in range(2):
+                scaled(yg, t, h)
+            nc.sync.dma_start(yg2[t][:], yg[t][:])
+        for t in range(PACK):
+            for h in range(2):
+                nc.scalar.copy(y[t][:, cols(h)], y_psum(t, h))
+        w2g = dealt("w2g", w2_raw, nc.scalar.copy)
+
+        def add_turned(dst, t, first, second):
+            c = slice(t * P, (t + 1) * P)
+            nc.tensor.matmul(dst[:, c], first, ident[:], start=True, stop=False, is_transpose=True)
+            nc.tensor.matmul(dst[:, c], second, ident[:], start=False, stop=True, is_transpose=True)
+
+        def turn_back(name, sums, back):
+            for i in range(2):
+                rows = keep.tile([P, H], BF16, name="%s_r%d" % (name, i), align_bytes=64)
+                nc.scalar.copy(
+                    rows[:].rearrange("s (u p e) -> s u p e", u=2, e=2),
+                    sums[i][:].rearrange("s (u e p) -> s u p e", u=2, e=2),
+                )
+                words = rows[:].bitcast(F32)
+                for u in range(2):
+                    o = u * HALF + i * P
+                    nc.tensor.transpose(back[:, o : o + P], words[:, u * P : (u + 1) * P], ident[:])
+            grouped = keep.tile([P, PACK * HALF], BF16, name=name + "_g", align_bytes=64)
+            nc.scalar.copy(
+                grouped[:].bitcast(F32).rearrange("p (s u) -> p s u", u=2),
+                back[:].rearrange("p (u s) -> p s u", u=2),
+            )
+            return grouped
+
+        u_ = f32_tiles("u", S)
+        v_ = f32_tiles("v", S)
+        lo = f32_tiles("lo", S)
+        r_ = f32_tiles("r", S)
+        zsum = [bank(4 + i) for i in range(4)]
+
+        def clamp_hi(t):
+            nc.vector.scalar_tensor_tensor(lo[t][:], u_[t][:], 0.0, v_[t][:], ALU.max, ALU.min)
+
+        def clamp_lo(t):
+            nc.vector.scalar_tensor_tensor(r_[t][:], u_[t][:], 0.0, lo[t][:], ALU.min, ALU.max)
+            for i in range(4):
+                c = slice(i * P, (i + 1) * P)
+                add_turned(zsum[i], t, yg2[t][:, c], r_[t][:, c])
+
+        def diff(dst, win, lst, other, t, h):
+            nc.vector.tensor_tensor(dst[t][:, cols(h)], win[t][:].indirect(entries(lst, h)), other[t][:, cols(h)], ALU.subtract)
+
+        for t in range(PACK):
+            diff(u_, yg, l1, yg2, t, 0)
+            if t > 0:
+                clamp_hi(t - 1)
+            diff(v_, yg, l2, yg2, t, 0)
+            if t > 0:
+                clamp_lo(t - 1)
+            diff(u_, yg, l1, yg2, t, 1)
+            diff(v_, yg, l2, yg2, t, 1)
+
+        sg = f32_tiles("sg", S)
+        cg = f32_tiles("cg", S)
+        g3 = f32_tiles("g3", S)
+        g5 = f32_tiles("g5", S)
+
+        def gates(h):
+            for t in range(PACK):
+                nc.scalar.activation(sg[t][:, cols(h)], y[t][:].indirect(entries(l4, h)), ACT.Sigmoid)
+                nc.scalar.activation(cg[t][:, cols(h)], sg[t][:, cols(h)], ACT.Copy, scale=-1.0, bias=1.0)
+
+        def times(dst, lst, other, t, h):
+            nc.vector.tensor_tensor(dst[t][:, cols(h)], yg[t][:].indirect(entries(lst, h)), other[t][:, cols(h)], ALU.mult)
+
+        def lerp(t, h, sums):
+            times(g5, l5, sg, t, h)
+            times(g3, l3, cg, t, h)
+            for i in range(2):
+                c = slice(h * HALF + i * P, h * HALF + (i + 1) * P)
+                add_turned(sums[i], t, g5[t][:, c], g3[t][:, c])
+
+        gates(0)
+        sums0 = [bank(2), bank(3)]
+        times(g5, l5, sg, 0, 0)
+        clamp_hi(3)
+        times(g3, l3, cg, 0, 0)
+        clamp_lo(3)
+        for i in range(2):
+            c = slice(i * P, (i + 1) * P)
+            add_turned(sums0[i], 0, g5[0][:, c], g3[0][:, c])
+        w2q = quantize("w2q", w2g[:], H)
+        gates(1)
+        zg = [turn_back("z%d" % h, zsum[2 * h : 2 * h + 2], bank(h)) for h in range(2)]
+        for t in range(1, PACK):
+            lerp(t, 0, sums0)
+
+        a = f32_tiles("a", S)
+        a2 = f32_tiles("ac", S)
+        b = f32_tiles("b", S)
+        b2 = f32_tiles("bc", S)
+        zq = [quantize("zq%d" % h, zg[h][:], HALF) for h in range(2)]
+        for t in range(PACK):
+            abank = bank(4 + t)
+            for h in range(2):
+                product(abank[:, cols(h)], w2q, t, zq[h][0][:], zq[h][1][:])
+            nc.scalar.copy(a[t][:], abank[:])
+            nc.sync.dma_start(a2[t][:], a[t][:])
+
+        z2g0 = turn_back("z20", sums0, bank(0))
+        sums1 = [bank(2), bank(3)]
+        for t in range(2):
+            lerp(t, 1, sums1)
+        z2q0 = quantize("z2q0", z2g0[:], HALF)
+        bb = [bank(4), bank(5)]
+        for t in range(PACK):
+            product(bb[t // 2][:, cols(t % 2)], w2q, t, z2q0[0][:], z2q0[1][:])
+        for t in range(PACK):
+            nc.scalar.copy(b[t][:, cols(0)], bb[t // 2][:, cols(t % 2)])
+            nc.sync.dma_start(b2[t][:, cols(0)], b[t][:, cols(0)])
+        for t in range(2, PACK):
+            lerp(t, 1, sums1)
+        z2g1 = turn_back("z21", sums1, bank(1))
+
+        d = f32_tiles("d", S)
+        for t in range(2):
+            for h in range(2):
+                diff(d, a, l6, a2, t, h)
+        z2q1 = quantize("z2q1", z2g1[:], HALF)
+        bb = [bank(6), bank(7)]
+        for t in range(PACK):
+            product(bb[t // 2][:, cols(t % 2)], w2q, t, z2q1[0][:], z2q1[1][:])
+        for t in range(PACK):
+            nc.scalar.copy(b[t][:, cols(1)], bb[t // 2][:, cols(t % 2)])
+            nc.scalar.copy(b2[t][:, cols(1)], bb[t // 2][:, cols(t % 2)])
+        for t in range(2, PACK):
+            for h in range(2):
+                diff(d, a, l6, a2, t, h)
+
+        x_ = f32_tiles("x", S)
+        s_ = f32_tiles("s", S)
+        m_ = f32_tiles("m", S)
+        o_ = f32_tiles("o", S)
+        out_rows = out.rearrange("(p t) s -> p t s", t=PACK)
+
+        def gate(t, h):
+            diff(x_, b, l7, b2, t, h)
+            nc.scalar.activation(s_[t][:, cols(h)], x_[t][:, cols(h)], ACT.Sigmoid)
+
+        def pull(t, c):
+            nc.vector.tensor_tensor(m_[t][:, c], s_[t][:, c], d[t][:, c], ALU.mult)
+
+        def finish(t, c):
+            nc.vector.tensor_tensor(o_[t][:, c], m_[t][:, c], a[t][:, c], ALU.add)
+            nc.sync.dma_start(out_rows[:, t, c], o_[t][:, c])
+
+        whole = slice(0, S)
+        for t in range(PACK):
+            gate(t, 0)
+            if t > 0:
+                pull(t - 1, whole)
+            gate(t, 1)
+            if t > 0:
+                finish(t - 1, whole)
+        pull(3, cols(0))
+        pull(3, cols(1))
+        finish(3, cols(0))
+        finish(3, cols(1))

@@ -52,15 +52,14 @@ def tile_picked_tiepullbmedlerp_none_p_kernel(
 
         warm = keep.tile([P, 1], F32, name="warm")
         warm2 = keep.tile([P, 1], F32, name="warm2")
-        nc.vector.memset(warm[:], 0.0)
-        nc.scalar.activation(warm2[:], warm[:], ACT.Sigmoid)
-
         xs = keep.tile([P, T], U8, name="xs", align_bytes=64)
-        nc.vector.memset(xs[:].bitcast(I32), 0)
+        nc.gpsimd.memset(xs[:].bitcast(I32), 0)
         w1_raw = keep.tile([P, PACK, H], F32, name="w1_raw")
         nc.sync.dma_start(w1_raw[:], w1.rearrange("(p j) c -> p j c", j=PACK))
         for q in range(4):
-            nc.scalar.dma_start(xs[32 * q : 32 * q + 4, :].bitcast(I32), x_scales[0, 4 * q : 4 * q + 4, :].bitcast(I32))
+            nc.sync.dma_start(xs[32 * q : 32 * q + 4, :].bitcast(I32), x_scales[0, 4 * q : 4 * q + 4, :].bitcast(I32))
+        nc.vector.memset(warm[:], 0.0)
+        nc.scalar.activation(warm2[:], warm[:], ACT.Sigmoid)
         l_offs = load_list("l_offs", offs)
         xw = keep.tile([P, T], U32, name="xw", align_bytes=64)
         nc.sync.dma_start(xw[:].bitcast(I32), x_words[0].rearrange("p n t -> p (n t)").bitcast(I32))
@@ -76,6 +75,9 @@ def tile_picked_tiepullbmedlerp_none_p_kernel(
         l6 = load_list("l6", n6)
         l7 = load_list("l7", n7)
 
+        yg = f32_tiles("yg", 2 * S)
+        for t in range(PACK):
+            nc.gpsimd.memset(yg[t][:, S:], 0.0)
         ident = keep.tile([P, P], F32, name="ident")
         make_identity(nc, ident[:])
 
@@ -105,45 +107,42 @@ def tile_picked_tiepullbmedlerp_none_p_kernel(
         nc.vector.tensor_copy(xs_g[:], xs[:].indirect(l_offs[:]))
 
         ybank = [bank(i) for i in range(4)]
-        for h in range(2):
-            xw_g = keep.tile([P, HALF], U32, name="xw_g%d" % h, align_bytes=64)
-            nc.vector.tensor_copy(xw_g[:], xw[:].indirect(entries(l_offs, h)))
-            for t in range(PACK):
-                product(ybank[2 * h + t // 2][:, cols(t % 2)], w1q, t, xw_g[:], xs_g[:, cols(h)])
+        pieces = [(cols(0), ybank[0]), (cols(1), bank(7))]
+        xw_g = keep.tile([P, S], U32, name="xw_g", align_bytes=64)
+        for c, dst in pieces:
+            nc.vector.tensor_copy(xw_g[:, c], xw[:].indirect(l_offs[:, c.start // 16 : c.stop // 16]))
+            product(dst[:, c], w1q, 0, xw_g[:, c], xs_g[:, c])
+        for t in range(1, PACK):
+            product(ybank[t][:], w1q, t, xw_g[:], xs_g[:])
 
-        yg = f32_tiles("yg", S)
         yg2 = f32_tiles("ygc", S)
         y = f32_tiles("y", S)
 
-        def y_psum(t, h):
-            return ybank[2 * h + t // 2][:, cols(t % 2)]
+        def scaled(dst, src, t):
+            nc.scalar.activation(dst, src, ACT.Copy, scale=gain[:, t : t + 1])
 
-        def scaled(dst, t, h):
-            nc.scalar.activation(dst[t][:, cols(h)], y_psum(t, h), ACT.Copy, scale=gain[:, t : t + 1])
-
-        scaled(yg, 0, 0)
-        scaled(yg2, 0, 0)
-        scaled(yg, 0, 1)
-        scaled(yg2, 0, 1)
-        for h in range(2):
-            scaled(yg, 1, h)
-        for h in range(2):
-            scaled(yg2, 1, h)
+        for c, src in pieces:
+            scaled(yg[0][:, c], src[:, c], 0)
+            if c.start == 0:
+                scaled(yg2[0][:, c], src[:, c], 0)
+        for c, src in pieces[1:]:
+            scaled(yg2[0][:, c], src[:, c], 0)
+        scaled(yg[1][:, :S], ybank[1][:], 1)
+        scaled(yg2[1][:], ybank[1][:], 1)
         for t in (2, 3):
-            for h in range(2):
-                scaled(yg, t, h)
-            nc.sync.dma_start(yg2[t][:], yg[t][:])
-        for t in range(PACK):
-            for h in range(2):
-                nc.scalar.copy(y[t][:, cols(h)], y_psum(t, h))
-        w2g = dealt("w2g", w2_raw, nc.scalar.copy)
+            scaled(yg[t][:, :S], ybank[t][:], t)
+            nc.sync.dma_start(yg2[t][:], yg[t][:, :S])
+        for c, src in reversed(pieces):
+            nc.scalar.copy(y[0][:, c], src[:, c])
+        for t in range(1, PACK):
+            nc.scalar.copy(y[t][:], ybank[t][:])
 
         def add_turned(dst, t, first, second):
             c = slice(t * P, (t + 1) * P)
             nc.tensor.matmul(dst[:, c], first, ident[:], start=True, stop=False, is_transpose=True)
             nc.tensor.matmul(dst[:, c], second, ident[:], start=False, stop=True, is_transpose=True)
 
-        def turn_back(name, sums, back):
+        def turn_back(name, sums, back, grouped):
             for i in range(2):
                 rows = keep.tile([P, H], BF16, name="%s_r%d" % (name, i), align_bytes=64)
                 nc.scalar.copy(
@@ -154,24 +153,24 @@ def tile_picked_tiepullbmedlerp_none_p_kernel(
                 for u in range(2):
                     o = u * HALF + i * P
                     nc.tensor.transpose(back[:, o : o + P], words[:, u * P : (u + 1) * P], ident[:])
-            grouped = keep.tile([P, PACK * HALF], BF16, name=name + "_g", align_bytes=64)
             nc.scalar.copy(
-                grouped[:].bitcast(F32).rearrange("p (s u) -> p s u", u=2),
+                grouped.bitcast(F32).rearrange("p (s u) -> p s u", u=2),
                 back[:].rearrange("p (u s) -> p s u", u=2),
             )
-            return grouped
 
-        u_ = f32_tiles("u", S)
-        v_ = f32_tiles("v", S)
-        lo = f32_tiles("lo", S)
+        a = f32_tiles("a", 2 * S)
+        b = f32_tiles("b", 2 * S)
+        u_ = [keep.tile([P, S], F32, name="u%d" % t, tag="u%d" % t, align_bytes=64) for t in range(PACK)]
+        v_ = [b[t][:, S:] for t in range(PACK)]
+        lo = [a[t][:, S:] for t in range(PACK)]
         r_ = f32_tiles("r", S)
         zsum = [bank(4 + i) for i in range(4)]
 
         def clamp_hi(t):
-            nc.vector.scalar_tensor_tensor(lo[t][:], u_[t][:], 0.0, v_[t][:], ALU.max, ALU.min)
+            nc.vector.scalar_tensor_tensor(lo[t], u_[t][:], 0.0, v_[t], ALU.max, ALU.min)
 
         def clamp_lo(t):
-            nc.vector.scalar_tensor_tensor(r_[t][:], u_[t][:], 0.0, lo[t][:], ALU.min, ALU.max)
+            nc.vector.scalar_tensor_tensor(r_[t][:], u_[t][:], 0.0, lo[t], ALU.min, ALU.max)
             for i in range(4):
                 c = slice(i * P, (i + 1) * P)
                 add_turned(zsum[i], t, yg2[t][:, c], r_[t][:, c])
@@ -179,20 +178,21 @@ def tile_picked_tiepullbmedlerp_none_p_kernel(
         def diff(dst, win, lst, other, t, h):
             nc.vector.tensor_tensor(dst[t][:, cols(h)], win[t][:].indirect(entries(lst, h)), other[t][:, cols(h)], ALU.subtract)
 
-        for t in range(PACK):
-            diff(u_, yg, l1, yg2, t, 0)
-            if t > 0:
-                clamp_hi(t - 1)
-            diff(v_, yg, l2, yg2, t, 0)
-            if t > 0:
-                clamp_lo(t - 1)
-            diff(u_, yg, l1, yg2, t, 1)
-            diff(v_, yg, l2, yg2, t, 1)
+        def diff_all(dst, win, lst, other):
+            nc.vector.tensor_tensor(dst, win[:].indirect(lst[:]), other, ALU.subtract)
+
+        diff(u_, yg, l1, yg2, 0, 0)
+        diff(v_, yg, l2, yg2, 0, 0)
+        diff(u_, yg, l1, yg2, 0, 1)
+        diff(v_, yg, l2, yg2, 0, 1)
+        for t in range(1, PACK):
+            diff_all(u_[t][:], yg[t], l1, yg2[t][:])
+            clamp_hi(t - 1)
+            diff_all(v_[t], yg[t], l2, yg2[t][:])
+            clamp_lo(t - 1)
 
         sg = f32_tiles("sg", S)
         cg = f32_tiles("cg", S)
-        g3 = f32_tiles("g3", S)
-        g5 = f32_tiles("g5", S)
 
         def gates(h):
             for t in range(PACK):
@@ -200,71 +200,80 @@ def tile_picked_tiepullbmedlerp_none_p_kernel(
                 nc.scalar.activation(cg[t][:, cols(h)], sg[t][:, cols(h)], ACT.Copy, scale=-1.0, bias=1.0)
 
         def times(dst, lst, other, t, h):
-            nc.vector.tensor_tensor(dst[t][:, cols(h)], yg[t][:].indirect(entries(lst, h)), other[t][:, cols(h)], ALU.mult)
+            nc.vector.tensor_tensor(dst, yg[t][:].indirect(entries(lst, h)), other[t][:, cols(h)], ALU.mult)
 
-        def lerp(t, h, sums):
-            times(g5, l5, sg, t, h)
-            times(g3, l3, cg, t, h)
+        def add_pair(t, sums, pair):
             for i in range(2):
-                c = slice(h * HALF + i * P, h * HALF + (i + 1) * P)
-                add_turned(sums[i], t, g5[t][:, c], g3[t][:, c])
+                add_turned(sums[i], t, pair[:, i * P : (i + 1) * P], pair[:, HALF + i * P : HALF + (i + 1) * P])
 
+        def lerp(t, h, sums, pair):
+            times(pair[:, cols(0)], l5, sg, t, h)
+            times(pair[:, cols(1)], l3, cg, t, h)
+            add_pair(t, sums, pair)
+
+        pair0 = keep.tile([P, S], F32, name="pair0")
         gates(0)
-        sums0 = [bank(2), bank(3)]
-        times(g5, l5, sg, 0, 0)
+        w2g = dealt("w2g", w2_raw, nc.scalar.copy)
+        times(pair0[:, cols(0)], l5, sg, 0, 0)
         clamp_hi(3)
-        times(g3, l3, cg, 0, 0)
+        times(pair0[:, cols(1)], l3, cg, 0, 0)
         clamp_lo(3)
-        for i in range(2):
-            c = slice(i * P, (i + 1) * P)
-            add_turned(sums0[i], 0, g5[0][:, c], g3[0][:, c])
         w2q = quantize("w2q", w2g[:], H)
         gates(1)
-        zg = [turn_back("z%d" % h, zsum[2 * h : 2 * h + 2], bank(h)) for h in range(2)]
+        zg = keep.tile([P, PACK * S], BF16, name="zg", tag="zg", align_bytes=64)
+        for h in range(2):
+            turn_back("z%d" % h, zsum[2 * h : 2 * h + 2], bank(h), zg[:, h * PACK * HALF : (h + 1) * PACK * HALF])
+        sums0 = [bank(7), bank(1)]
+        add_pair(0, sums0, pair0[:])
+        after_z = keep.tile([P, 3 * S], F32, name="after_z", tag="u3", align_bytes=64)
         for t in range(1, PACK):
-            lerp(t, 0, sums0)
+            lerp(t, 0, sums0, after_z[:, (t - 1) * S : t * S])
+        z2g0 = keep.tile([P, PACK * HALF], BF16, name="z2g0", align_bytes=64)
+        turn_back("z20", sums0, bank(2), z2g0[:])
 
-        a = f32_tiles("a", S)
         a2 = f32_tiles("ac", S)
-        b = f32_tiles("b", S)
         b2 = f32_tiles("bc", S)
-        zq = [quantize("zq%d" % h, zg[h][:], HALF) for h in range(2)]
+        pair1 = keep.tile([P, S], F32, name="pair_first")
+        times(pair1[:, cols(0)], l5, sg, 0, 1)
+        times(pair1[:, cols(1)], l3, cg, 0, 1)
+        zq = quantize("zq", zg[:], S)
         for t in range(PACK):
-            abank = bank(4 + t)
-            for h in range(2):
-                product(abank[:, cols(h)], w2q, t, zq[h][0][:], zq[h][1][:])
-            nc.scalar.copy(a[t][:], abank[:])
-            nc.sync.dma_start(a2[t][:], a[t][:])
+            abank = bank((4, 5, 6, 0)[t])
+            product(abank[:], w2q, t, zq[0][:], zq[1][:])
+            nc.scalar.copy(a[t][:, :S], abank[:])
+            if t == 0:
+                nc.scalar.copy(a2[t][:], abank[:])
+            else:
+                nc.sync.dma_start(a2[t][:], a[t][:, :S])
+        sums1 = [bank(4), bank(5)]
+        add_pair(0, sums1, pair1[:])
+        after_zq = keep.tile([P, 3 * S], F32, name="after_zq", tag="zg", align_bytes=64)
+        for t in range(1, PACK):
+            lerp(t, 1, sums1, after_zq[:, (t - 1) * S : t * S])
+        z2g1 = keep.tile([P, PACK * HALF], BF16, name="z2g1", tag="z2g1", align_bytes=64)
+        turn_back("z21", sums1, bank(0), z2g1[:])
 
-        z2g0 = turn_back("z20", sums0, bank(0))
-        sums1 = [bank(2), bank(3)]
-        for t in range(2):
-            lerp(t, 1, sums1)
+        d = [keep.tile([P, S], F32, name="d%d" % t) for t in range(3)]
+        bbank = [bank(i) for i in (3, 7, 1, 2)]
         z2q0 = quantize("z2q0", z2g0[:], HALF)
-        bb = [bank(4), bank(5)]
         for t in range(PACK):
-            product(bb[t // 2][:, cols(t % 2)], w2q, t, z2q0[0][:], z2q0[1][:])
-        for t in range(PACK):
-            nc.scalar.copy(b[t][:, cols(0)], bb[t // 2][:, cols(t % 2)])
-            nc.sync.dma_start(b2[t][:, cols(0)], b[t][:, cols(0)])
-        for t in range(2, PACK):
-            lerp(t, 1, sums1)
-        z2g1 = turn_back("z21", sums1, bank(1))
-
-        d = f32_tiles("d", S)
+            product(bbank[t][:, cols(0)], w2q, t, z2q0[0][:], z2q0[1][:])
         for t in range(2):
-            for h in range(2):
-                diff(d, a, l6, a2, t, h)
+            diff_all(d[t][:], a[t], l6, a2[t][:])
+        diff(d, a, l6, a2, 2, 0)
         z2q1 = quantize("z2q1", z2g1[:], HALF)
-        bb = [bank(6), bank(7)]
         for t in range(PACK):
-            product(bb[t // 2][:, cols(t % 2)], w2q, t, z2q1[0][:], z2q1[1][:])
-        for t in range(PACK):
-            nc.scalar.copy(b[t][:, cols(1)], bb[t // 2][:, cols(t % 2)])
-            nc.scalar.copy(b2[t][:, cols(1)], bb[t // 2][:, cols(t % 2)])
-        for t in range(2, PACK):
-            for h in range(2):
-                diff(d, a, l6, a2, t, h)
+            product(bbank[t][:, cols(1)], w2q, t, z2q1[0][:], z2q1[1][:])
+        after_z2q1 = keep.tile([P, S + HALF], F32, name="after_z2q1", tag="z2g1", align_bytes=64)
+        d2_late = after_z2q1[:, S:]
+        nc.vector.tensor_tensor(d2_late, a[2][:].indirect(entries(l6, 1)), a2[2][:, cols(1)], ALU.subtract)
+        d.append(after_z2q1)
+        diff_all(d[3][:, :S], a[3], l6, a2[3][:])
+
+        def b_out(t):
+            nc.scalar.copy(b[t][:, :S], bbank[t][:])
+            nc.scalar.copy(b2[t][:], bbank[t][:])
+
 
         x_ = f32_tiles("x", S)
         s_ = f32_tiles("s", S)
@@ -277,21 +286,32 @@ def tile_picked_tiepullbmedlerp_none_p_kernel(
             nc.scalar.activation(s_[t][:, cols(h)], x_[t][:, cols(h)], ACT.Sigmoid)
 
         def pull(t, c):
-            nc.vector.tensor_tensor(m_[t][:, c], s_[t][:, c], d[t][:, c], ALU.mult)
+            if t == 2:
+                nc.vector.tensor_tensor(m_[t][:, cols(0)], s_[t][:, cols(0)], d[t][:, cols(0)], ALU.mult)
+                nc.vector.tensor_tensor(m_[t][:, cols(1)], s_[t][:, cols(1)], d2_late, ALU.mult)
+            else:
+                nc.vector.tensor_tensor(m_[t][:, c], s_[t][:, c], d[t][:, c], ALU.mult)
 
         def finish(t, c):
             nc.vector.tensor_tensor(o_[t][:, c], m_[t][:, c], a[t][:, c], ALU.add)
             nc.sync.dma_start(out_rows[:, t, c], o_[t][:, c])
 
         whole = slice(0, S)
-        for t in range(PACK):
-            gate(t, 0)
-            if t > 0:
-                pull(t - 1, whole)
-            gate(t, 1)
-            if t > 0:
-                finish(t - 1, whole)
+        b_out(0)
+        for t in range(3):
+            b_out(t + 1)
+            diff_all(x_[t][:], b[t], l7, b2[t][:])
+            nc.scalar.activation(s_[t][:], x_[t][:], ACT.Sigmoid)
+            if t == 1:
+                pull(0, whole)
+        finish(0, whole)
+        pull(1, whole)
+        gate(3, 0)
+        finish(1, whole)
+        gate(3, 1)
+        pull(2, whole)
         pull(3, cols(0))
+        finish(2, whole)
         pull(3, cols(1))
         finish(3, cols(0))
         finish(3, cols(1))

@@ -237,14 +237,15 @@ def tile_picked_tiepullbmedlerp_none_p_kernel(
         times(pair1[:, cols(0)], l5, sg, 0, 1)
         times(pair1[:, cols(1)], l3, cg, 0, 1)
         zq = quantize("zq", zg[:], S)
+        abank = [bank(i) for i in (4, 5, 6, 0)]
         for t in range(PACK):
-            abank = bank((4, 5, 6, 0)[t])
-            product(abank[:], w2q, t, zq[0][:], zq[1][:])
-            nc.scalar.copy(a[t][:, :S], abank[:])
-            if t == 0:
-                nc.scalar.copy(a2[t][:], abank[:])
-            else:
+            product(abank[t][:], w2q, t, zq[0][:], zq[1][:])
+        for t in range(PACK):
+            nc.scalar.copy(a[t][:, :S], abank[t][:])
+            if t > 0:
                 nc.sync.dma_start(a2[t][:], a[t][:, :S])
+            if t == 1:
+                nc.scalar.copy(a2[0][:], abank[0][:])
         sums1 = [bank(4), bank(5)]
         add_pair(0, sums1, pair1[:])
         after_zq = keep.tile([P, 3 * S], F32, name="after_zq", tag="zg", align_bytes=64)
@@ -253,17 +254,27 @@ def tile_picked_tiepullbmedlerp_none_p_kernel(
         z2g1 = keep.tile([P, PACK * HALF], BF16, name="z2g1", tag="z2g1", align_bytes=64)
         turn_back("z21", sums1, bank(0), z2g1[:])
 
-        d = [keep.tile([P, S], F32, name="d%d" % t) for t in range(3)]
-        bbank = [bank(i) for i in (3, 7, 1, 2)]
+        d = [keep.tile([P, S], F32, name="d%d" % t, tag="d%d" % t, align_bytes=64) for t in range(3)]
+        bbank = [[bank(3), bank(7)], [bank(1), bank(2)]]
+
+        def b_psum(t, h):
+            return bbank[h][t // 2][:, cols(t % 2)]
+
         z2q0 = quantize("z2q0", z2g0[:], HALF)
         for t in range(PACK):
-            product(bbank[t][:, cols(0)], w2q, t, z2q0[0][:], z2q0[1][:])
+            product(b_psum(t, 0), w2q, t, z2q0[0][:], z2q0[1][:])
+        for t in range(PACK):
+            nc.scalar.copy(b[t][:, cols(0)], b_psum(t, 0))
+            if t < 2:
+                nc.scalar.copy(b2[t][:, cols(0)], b_psum(t, 0))
+            else:
+                nc.sync.dma_start(b2[t][:, cols(0)], b[t][:, cols(0)])
         for t in range(2):
             diff_all(d[t][:], a[t], l6, a2[t][:])
         diff(d, a, l6, a2, 2, 0)
         z2q1 = quantize("z2q1", z2g1[:], HALF)
         for t in range(PACK):
-            product(bbank[t][:, cols(1)], w2q, t, z2q1[0][:], z2q1[1][:])
+            product(b_psum(t, 1), w2q, t, z2q1[0][:], z2q1[1][:])
         after_z2q1 = keep.tile([P, S + HALF], F32, name="after_z2q1", tag="z2g1", align_bytes=64)
         d2_late = after_z2q1[:, S:]
         nc.vector.tensor_tensor(d2_late, a[2][:].indirect(entries(l6, 1)), a2[2][:, cols(1)], ALU.subtract)
@@ -271,13 +282,13 @@ def tile_picked_tiepullbmedlerp_none_p_kernel(
         diff_all(d[3][:, :S], a[3], l6, a2[3][:])
 
         def b_out(t):
-            nc.scalar.copy(b[t][:, :S], bbank[t][:])
-            nc.scalar.copy(b2[t][:], bbank[t][:])
+            nc.scalar.copy(b[t][:, cols(1)], b_psum(t, 1))
+            nc.scalar.copy(b2[t][:, cols(1)], b_psum(t, 1))
 
 
-        x_ = f32_tiles("x", S)
-        s_ = f32_tiles("s", S)
-        m_ = f32_tiles("m", S)
+        x_ = {t: keep.tile([P, S], F32, name="x%d" % t) for t in (0, 1, 3)}
+        s_ = {t: keep.tile([P, S], F32, name="s%d" % t) for t in (0, 1, 3)}
+        m_ = [keep.tile([P, S], F32, name="m%d" % t, tag="m%d" % t, align_bytes=64) for t in range(PACK)]
         o_ = f32_tiles("o", S)
         out_rows = out.rearrange("(p t) s -> p t s", t=PACK)
 
@@ -296,15 +307,34 @@ def tile_picked_tiepullbmedlerp_none_p_kernel(
             nc.vector.tensor_tensor(o_[t][:, c], m_[t][:, c], a[t][:, c], ALU.add)
             nc.sync.dma_start(out_rows[:, t, c], o_[t][:, c])
 
-        whole = slice(0, S)
-        b_out(0)
-        for t in range(3):
-            b_out(t + 1)
+        def finish_turned(t, sums, back):
+            for i in range(4):
+                c = slice(i * P, (i + 1) * P)
+                add_turned(sums, i, a[t][:, c], m_[t][:, c])
+            turned = keep.tile([P, S], F32, name="turned%d" % t)
+            nc.scalar.copy(turned[:], sums[:])
+            for i in range(4):
+                c = slice(i * P, (i + 1) * P)
+                nc.tensor.transpose(back[:, c], turned[:, c], ident[:])
+            nc.scalar.copy(o_[t][:], back[:])
+            nc.sync.dma_start(out_rows[:, t, :], o_[t][:])
+
+        def gate_all(t):
             diff_all(x_[t][:], b[t], l7, b2[t][:])
             nc.scalar.activation(s_[t][:], x_[t][:], ACT.Sigmoid)
-            if t == 1:
-                pull(0, whole)
-        finish(0, whole)
+
+        whole = slice(0, S)
+        b_out(0)
+        b_out(1)
+        b_out(2)
+        gate_all(0)
+        b_out(3)
+        gate_all(1)
+        pull(0, whole)
+        finish_turned(0, bank(4), bank(5))
+        x_[2] = keep.tile([P, S], F32, name="x_late", tag="d0", align_bytes=64)
+        s_[2] = keep.tile([P, S], F32, name="s_late", tag="m0", align_bytes=64)
+        gate_all(2)
         pull(1, whole)
         gate(3, 0)
         finish(1, whole)

@@ -81,11 +81,11 @@ def tile_picked_tiepullbmedlerp_none_p_kernel(
         ident = keep.tile([P, P], F32, name="ident")
         make_identity(nc, ident[:])
 
-        def dealt(name, raw, copy):
-            grouped = keep.tile([P, PACK * H], BF16, name=name, align_bytes=64)
+        def dealt(name, raw, pair, copy):
+            grouped = keep.tile([P, 2 * H], BF16, name=name, align_bytes=64)
             copy(
-                grouped[:].rearrange("p (t m j) -> p m j t", t=PACK, j=PACK),
-                raw[:].rearrange("p j (m t) -> p m j t", t=PACK),
+                grouped[:].rearrange("p (t m j) -> p m j t", t=2, j=PACK),
+                raw[:].rearrange("p j (m t) -> p m j t", t=PACK)[:, :, :, 2 * pair : 2 * pair + 2],
             )
             return grouped
 
@@ -96,15 +96,17 @@ def tile_picked_tiepullbmedlerp_none_p_kernel(
             return codes, scales
 
         def product(dst, w, t, codes, scales):
-            m = slice(t * P, (t + 1) * P)
+            m = slice(t % 2 * P, (t % 2 + 1) * P)
+            w_codes, w_scales = w[t // 2]
             nc.tensor.matmul_mx(
-                out=dst, lhsT=w[0][:, m].bitcast(FP8X4), lhsT_scale=w[1][:, m],
+                out=dst, lhsT=w_codes[:, m].bitcast(FP8X4), lhsT_scale=w_scales[:, m],
                 rhs=codes.bitcast(FP8X4), rhs_scale=scales, start=True, stop=True,
             )
 
-        w1q = quantize("w1q", dealt("w1g", w1_raw, nc.vector.tensor_copy)[:], H)
+        w1g = [dealt("w1g0", w1_raw, 0, nc.vector.tensor_copy), dealt("w1g1", w1_raw, 1, nc.scalar.copy)]
         xs_g = keep.tile([P, S], U8, name="xs_g", align_bytes=64)
         nc.vector.tensor_copy(xs_g[:], xs[:].indirect(l_offs[:]))
+        w1q = [quantize("w1q%d" % i, w1g[i][:], 2 * P) for i in range(2)]
 
         ybank = [bank(i) for i in range(4)]
         pieces = [(cols(0), ybank[0]), (cols(1), bank(7))]
@@ -213,12 +215,12 @@ def tile_picked_tiepullbmedlerp_none_p_kernel(
 
         pair0 = keep.tile([P, S], F32, name="pair0")
         gates(0)
-        w2g = dealt("w2g", w2_raw, nc.scalar.copy)
+        w2g = [dealt("w2g%d" % i, w2_raw, i, nc.scalar.copy) for i in range(2)]
         times(pair0[:, cols(0)], l5, sg, 0, 0)
         clamp_hi(3)
         times(pair0[:, cols(1)], l3, cg, 0, 0)
         clamp_lo(3)
-        w2q = quantize("w2q", w2g[:], H)
+        w2q = [quantize("w2q%d" % i, w2g[i][:], 2 * P) for i in range(2)]
         gates(1)
         zg = keep.tile([P, PACK * S], BF16, name="zg", tag="zg", align_bytes=64)
         for h in range(2):

from contextlib import ExitStack

import concourse.mybir as mybir
from concourse.masks import make_identity

F32 = mybir.dt.float32
BF16 = mybir.dt.bfloat16
I32 = mybir.dt.int32
U32 = mybir.dt.uint32
U16 = mybir.dt.uint16
U8 = mybir.dt.uint8
FP8X4 = mybir.dt.float8_e4m3fn_x4
ALU = mybir.AluOpType
ACT = mybir.ActivationFunctionType

P = 128
PACK = 4
T = 2048
S = 512
H = 512
HALF = S // 2
FLOPS = 3 * 2 * 512 * 512 * 512


def cols(h):
    return slice(h * HALF, (h + 1) * HALF)


def entries(lst, h):
    return lst[:, h * (HALF // 16) : (h + 1) * (HALF // 16)]


def tile_picked_tiepullbmedlerp_none_p_kernel(
    tc, x_words, x_scales, w1, gn, w2, offs, n1, n2, n3, n4, n5, n6, n7, out
):
    nc = tc.nc
    with ExitStack() as ctx:
        lists = ctx.enter_context(tc.tile_pool(name="lists", bufs=1))
        keep = ctx.enter_context(tc.tile_pool(name="keep", bufs=1))
        psum = ctx.enter_context(tc.psum_pool(name="psum", bufs=1))

        def bank(i):
            return psum.tile([P, S], F32, name="bank%d" % i)

        def load_list(name, src):
            tile = lists.tile([P, S // 16], U16, name=name)
            nc.sync.dma_start(tile[:], src)
            return tile

        def f32_tiles(name, width):
            return [keep.tile([P, width], F32, name="%s%d" % (name, t), align_bytes=64) for t in range(PACK)]

        warm = keep.tile([P, 1], F32, name="warm")
        warm2 = keep.tile([P, 1], F32, name="warm2")
        xs = keep.tile([P, T], U8, name="xs", align_bytes=64)
        nc.gpsimd.memset(xs[:].bitcast(I32), 0)
        w1_raw = keep.tile([P, PACK, H], F32, name="w1_raw")
        nc.sync.dma_start(w1_raw[:], w1.rearrange("(p j) c -> p j c", j=PACK))
        for q in range(4):
            nc.sync.dma_start(xs[32 * q : 32 * q + 4, :].bitcast(I32), x_scales[0, 4 * q : 4 * q + 4, :].bitcast(I32))
        nc.vector.memset(warm[:], 0.0)
        nc.scalar.activation(warm2[:], warm[:], ACT.Sigmoid)
        l_offs = load_list("l_offs", offs)
        xw = keep.tile([P, T], U32, name="xw", align_bytes=64)
        nc.sync.dma_start(xw[:].bitcast(I32), x_words[0].rearrange("p n t -> p (n t)").bitcast(I32))
        gain = keep.tile([P, PACK], F32, name="gain")
        nc.sync.dma_start(gain[:], gn.rearrange("(p t) o -> p (t o)", t=PACK))
        l1 = load_list("l1", n1)
        l2 = load_list("l2", n2)
        w2_raw = keep.tile([P, PACK, H], F32, name="w2_raw")
        nc.sync.dma_start(w2_raw[:], w2.rearrange("(p j) c -> p j c", j=PACK))
        l4 = load_list("l4", n4)
        l3 = load_list("l3", n3)
        l5 = load_list("l5", n5)
        l6 = load_list("l6", n6)
        l7 = load_list("l7", n7)

        yg = f32_tiles("yg", 2 * S)
        for t in range(PACK):
            nc.gpsimd.memset(yg[t][:, S:], 0.0)
        ident = keep.tile([P, P], F32, name="ident")
        make_identity(nc, ident[:])

        def dealt(name, raw, pair, copy):
            grouped = keep.tile([P, 2 * H], BF16, name=name, align_bytes=64)
            copy(
                grouped[:].rearrange("p (t m j) -> p m j t", t=2, j=PACK),
                raw[:].rearrange("p j (m t) -> p m j t", t=PACK)[:, :, :, 2 * pair : 2 * pair + 2],
            )
            return grouped

        def quantize(name, grouped, width):
            codes = keep.tile([P, width], U32, name=name + "_c", align_bytes=64)
            scales = keep.tile([P, width], U8, name=name + "_s", align_bytes=64)
            nc.vector.quantize_mx(out=codes[:].bitcast(FP8X4), scales=scales[:], in_=grouped)
            return codes, scales

        def product(dst, w, t, codes, scales):
            m = slice(t % 2 * P, (t % 2 + 1) * P)
            w_codes, w_scales = w[t // 2]
            nc.tensor.matmul_mx(
                out=dst, lhsT=w_codes[:, m].bitcast(FP8X4), lhsT_scale=w_scales[:, m],
                rhs=codes.bitcast(FP8X4), rhs_scale=scales, start=True, stop=True,
            )

        w1g = [dealt("w1g0", w1_raw, 0, nc.vector.tensor_copy), dealt("w1g1", w1_raw, 1, nc.scalar.copy)]
        xs_g = keep.tile([P, S], U8, name="xs_g", align_bytes=64)
        nc.vector.tensor_copy(xs_g[:], xs[:].indirect(l_offs[:]))
        w1q = [quantize("w1q%d" % i, w1g[i][:], 2 * P) for i in range(2)]

        ybank = [bank(i) for i in range(4)]
        pieces = [(cols(0), ybank[0]), (cols(1), bank(7))]
        xw_g = keep.tile([P, S], U32, name="xw_g", align_bytes=64)
        for c, dst in pieces:
            nc.vector.tensor_copy(xw_g[:, c], xw[:].indirect(l_offs[:, c.start // 16 : c.stop // 16]))
            product(dst[:, c], w1q, 0, xw_g[:, c], xs_g[:, c])
        for t in range(1, PACK):
            product(ybank[t][:], w1q, t, xw_g[:], xs_g[:])

        yg2 = f32_tiles("ygc", S)
        y = f32_tiles("y", S)

        def scaled(dst, src, t):
            nc.scalar.activation(dst, src, ACT.Copy, scale=gain[:, t : t + 1])

        for c, src in pieces:
            scaled(yg[0][:, c], src[:, c], 0)
            if c.start == 0:
                scaled(yg2[0][:, c], src[:, c], 0)
        for c, src in pieces[1:]:
            scaled(yg2[0][:, c], src[:, c], 0)
        scaled(yg[1][:, :S], ybank[1][:], 1)
        scaled(yg2[1][:], ybank[1][:], 1)
        for t in (2, 3):
            scaled(yg[t][:, :S], ybank[t][:], t)
            nc.sync.dma_start(yg2[t][:], yg[t][:, :S])
        for c, src in reversed(pieces):
            nc.scalar.copy(y[0][:, c], src[:, c])
        for t in range(1, PACK):
            nc.scalar.copy(y[t][:], ybank[t][:])

        def add_turned(dst, t, first, second):
            c = slice(t * P, (t + 1) * P)
            nc.tensor.matmul(dst[:, c], first, ident[:], start=True, stop=False, is_transpose=True)
            nc.tensor.matmul(dst[:, c], second, ident[:], start=False, stop=True, is_transpose=True)

        def turn_back(name, sums, back, grouped):
            for i in range(2):
                rows = keep.tile([P, H], BF16, name="%s_r%d" % (name, i), align_bytes=64)
                nc.scalar.copy(
                    rows[:].rearrange("s (u p e) -> s u p e", u=2, e=2),
                    sums[i][:].rearrange("s (u e p) -> s u p e", u=2, e=2),
                )
                words = rows[:].bitcast(F32)
                for u in range(2):
                    o = u * HALF + i * P
                    nc.tensor.transpose(back[:, o : o + P], words[:, u * P : (u + 1) * P], ident[:])
            nc.scalar.copy(
                grouped.bitcast(F32).rearrange("p (s u) -> p s u", u=2),
                back[:].rearrange("p (u s) -> p s u", u=2),
            )

        a = f32_tiles("a", 2 * S)
        b = f32_tiles("b", 2 * S)
        u_ = [keep.tile([P, S], F32, name="u%d" % t, tag="u%d" % t, align_bytes=64) for t in range(PACK)]
        v_ = [b[t][:, S:] for t in range(PACK)]
        lo = [a[t][:, S:] for t in range(PACK)]
        r_ = f32_tiles("r", S)
        zsum = [bank(4 + i) for i in range(4)]

        def clamp_hi(t):
            nc.vector.scalar_tensor_tensor(lo[t], u_[t][:], 0.0, v_[t], ALU.max, ALU.min)

        def clamp_lo(t):
            nc.vector.scalar_tensor_tensor(r_[t][:], u_[t][:], 0.0, lo[t], ALU.min, ALU.max)
            for i in range(4):
                c = slice(i * P, (i + 1) * P)
                add_turned(zsum[i], t, yg2[t][:, c], r_[t][:, c])

        def diff(dst, win, lst, other, t, h):
            nc.vector.tensor_tensor(dst[t][:, cols(h)], win[t][:].indirect(entries(lst, h)), other[t][:, cols(h)], ALU.subtract)

        def diff_all(dst, win, lst, other):
            nc.vector.tensor_tensor(dst, win[:].indirect(lst[:]), other, ALU.subtract)

        diff(u_, yg, l1, yg2, 0, 0)
        diff(v_, yg, l2, yg2, 0, 0)
        diff(u_, yg, l1, yg2, 0, 1)
        diff(v_, yg, l2, yg2, 0, 1)
        for t in range(1, PACK):
            diff_all(u_[t][:], yg[t], l1, yg2[t][:])
            clamp_hi(t - 1)
            diff_all(v_[t], yg[t], l2, yg2[t][:])
            clamp_lo(t - 1)

        sg = f32_tiles("sg", S)
        cg = f32_tiles("cg", S)

        def gates(h):
            for t in range(PACK):
                nc.scalar.activation(sg[t][:, cols(h)], y[t][:].indirect(entries(l4, h)), ACT.Sigmoid)
                nc.scalar.activation(cg[t][:, cols(h)], sg[t][:, cols(h)], ACT.Copy, scale=-1.0, bias=1.0)

        def times(dst, lst, other, t, h):
            nc.vector.tensor_tensor(dst, yg[t][:].indirect(entries(lst, h)), other[t][:, cols(h)], ALU.mult)

        def add_pair(t, sums, pair):
            for i in range(2):
                add_turned(sums[i], t, pair[:, i * P : (i + 1) * P], pair[:, HALF + i * P : HALF + (i + 1) * P])

        def lerp(t, h, sums, pair):
            times(pair[:, cols(0)], l5, sg, t, h)
            times(pair[:, cols(1)], l3, cg, t, h)
            add_pair(t, sums, pair)

        pair0 = keep.tile([P, S], F32, name="pair0")
        gates(0)
        w2g = [dealt("w2g%d" % i, w2_raw, i, nc.scalar.copy) for i in range(2)]
        times(pair0[:, cols(0)], l5, sg, 0, 0)
        clamp_hi(3)
        times(pair0[:, cols(1)], l3, cg, 0, 0)
        clamp_lo(3)
        w2q = [quantize("w2q%d" % i, w2g[i][:], 2 * P) for i in range(2)]
        gates(1)
        zg = keep.tile([P, PACK * S], BF16, name="zg", tag="zg", align_bytes=64)
        for h in range(2):
            turn_back("z%d" % h, zsum[2 * h : 2 * h + 2], bank(h), zg[:, h * PACK * HALF : (h + 1) * PACK * HALF])
        sums0 = [bank(7), bank(1)]
        add_pair(0, sums0, pair0[:])
        after_z = keep.tile([P, 3 * S], F32, name="after_z", tag="u3", align_bytes=64)
        for t in range(1, PACK):
            lerp(t, 0, sums0, after_z[:, (t - 1) * S : t * S])
        z2g0 = keep.tile([P, PACK * HALF], BF16, name="z2g0", align_bytes=64)
        turn_back("z20", sums0, bank(2), z2g0[:])

        a2 = f32_tiles("ac", S)
        b2 = f32_tiles("bc", S)
        pair1 = keep.tile([P, S], F32, name="pair_first")
        times(pair1[:, cols(0)], l5, sg, 0, 1)
        times(pair1[:, cols(1)], l3, cg, 0, 1)
        zq = quantize("zq", zg[:], S)
        abank = [bank(i) for i in (4, 5, 6, 0)]
        for t in range(PACK):
            product(abank[t][:], w2q, t, zq[0][:], zq[1][:])
        for t in range(PACK):
            nc.scalar.copy(a[t][:, :S], abank[t][:])
            if t > 0:
                nc.sync.dma_start(a2[t][:], a[t][:, :S])
            if t == 1:
                nc.scalar.copy(a2[0][:], abank[0][:])
        sums1 = [bank(4), bank(5)]
        add_pair(0, sums1, pair1[:])
        after_zq = keep.tile([P, 3 * S], F32, name="after_zq", tag="zg", align_bytes=64)
        for t in range(1, PACK):
            lerp(t, 1, sums1, after_zq[:, (t - 1) * S : t * S])
        z2g1 = keep.tile([P, PACK * HALF], BF16, name="z2g1", tag="z2g1", align_bytes=64)
        turn_back("z21", sums1, bank(0), z2g1[:])

        d = [keep.tile([P, S], F32, name="d%d" % t, tag="d%d" % t, align_bytes=64) for t in range(3)]
        bbank = [[bank(3), bank(7)], [bank(1), bank(2)]]

        def b_psum(t, h):
            return bbank[h][t // 2][:, cols(t % 2)]

        z2q0 = quantize("z2q0", z2g0[:], HALF)
        for t in range(PACK):
            product(b_psum(t, 0), w2q, t, z2q0[0][:], z2q0[1][:])
        for t in range(PACK):
            nc.scalar.copy(b[t][:, cols(0)], b_psum(t, 0))
            if t < 2:
                nc.scalar.copy(b2[t][:, cols(0)], b_psum(t, 0))
            else:
                nc.sync.dma_start(b2[t][:, cols(0)], b[t][:, cols(0)])
        for t in range(2):
            diff_all(d[t][:], a[t], l6, a2[t][:])
        diff(d, a, l6, a2, 2, 0)
        z2q1 = quantize("z2q1", z2g1[:], HALF)
        for t in range(PACK):
            product(b_psum(t, 1), w2q, t, z2q1[0][:], z2q1[1][:])
        after_z2q1 = keep.tile([P, S + HALF], F32, name="after_z2q1", tag="z2g1", align_bytes=64)
        d2_late = after_z2q1[:, S:]
        nc.vector.tensor_tensor(d2_late, a[2][:].indirect(entries(l6, 1)), a2[2][:, cols(1)], ALU.subtract)
        d.append(after_z2q1)
        diff_all(d[3][:, :S], a[3], l6, a2[3][:])

        def b_out(t):
            nc.scalar.copy(b[t][:, cols(1)], b_psum(t, 1))
            nc.scalar.copy(b2[t][:, cols(1)], b_psum(t, 1))


        x_ = {t: keep.tile([P, S], F32, name="x%d" % t) for t in (0, 1, 3)}
        s_ = {t: keep.tile([P, S], F32, name="s%d" % t) for t in (0, 1, 3)}
        m_ = [keep.tile([P, S], F32, name="m%d" % t, tag="m%d" % t, align_bytes=64) for t in range(PACK)]
        o_ = f32_tiles("o", S)
        out_rows = out.rearrange("(p t) s -> p t s", t=PACK)

        def gate(t, h):
            diff(x_, b, l7, b2, t, h)
            nc.scalar.activation(s_[t][:, cols(h)], x_[t][:, cols(h)], ACT.Sigmoid)

        def pull(t, c):
            if t == 2:
                nc.vector.tensor_tensor(m_[t][:, cols(0)], s_[t][:, cols(0)], d[t][:, cols(0)], ALU.mult)
                nc.vector.tensor_tensor(m_[t][:, cols(1)], s_[t][:, cols(1)], d2_late, ALU.mult)
            else:
                nc.vector.tensor_tensor(m_[t][:, c], s_[t][:, c], d[t][:, c], ALU.mult)

        def finish(t, c):
            nc.vector.tensor_tensor(o_[t][:, c], m_[t][:, c], a[t][:, c], ALU.add)
            nc.sync.dma_start(out_rows[:, t, c], o_[t][:, c])

        def finish_turned(t, sums, back):
            for i in range(4):
                c = slice(i * P, (i + 1) * P)
                add_turned(sums, i, a[t][:, c], m_[t][:, c])
            turned = keep.tile([P, S], F32, name="turned%d" % t)
            nc.scalar.copy(turned[:], sums[:])
            for i in range(4):
                c = slice(i * P, (i + 1) * P)
                nc.tensor.transpose(back[:, c], turned[:, c], ident[:])
            nc.scalar.copy(o_[t][:], back[:])
            nc.sync.dma_start(out_rows[:, t, :], o_[t][:])

        def gate_all(t):
            diff_all(x_[t][:], b[t], l7, b2[t][:])
            nc.scalar.activation(s_[t][:], x_[t][:], ACT.Sigmoid)

        whole = slice(0, S)
        b_out(0)
        b_out(1)
        b_out(2)
        gate_all(0)
        b_out(3)
        gate_all(1)
        pull(0, whole)
        finish_turned(0, bank(4), bank(5))
        x_[2] = keep.tile([P, S], F32, name="x_late", tag="d0", align_bytes=64)
        s_[2] = keep.tile([P, S], F32, name="s_late", tag="m0", align_bytes=64)
        gate_all(2)
        pull(1, whole)
        gate(3, 0)
        finish(1, whole)
        gate(3, 1)
        pull(2, whole)
        pull(3, cols(0))
        finish(2, whole)
        pull(3, cols(1))
        finish(3, cols(0))
        finish(3, cols(1))
